import numpy as np
import ml_dtypes


def mxq(x, axis, fmt="e4m3"):
    dtype, down = {"e4m3": (ml_dtypes.float8_e4m3fn, 7), "e5m2": (ml_dtypes.float8_e5m2, 14)}[fmt]
    v = np.moveaxis(np.asarray(x, np.float32).astype(ml_dtypes.bfloat16).astype(np.float64), axis, -1)
    blocks = v.reshape(v.shape[:-1] + (-1, 32))
    amax = np.abs(blocks).max(-1, keepdims=True)
    byte = np.maximum(np.where(amax > 0, np.frexp(amax)[1] - 1 + 127, 0) - down, 1)
    scale = np.exp2(byte - 127.0)
    codes = (blocks / scale).astype(np.float32).astype(dtype).astype(np.float64)
    return np.moveaxis((codes * scale).reshape(v.shape), -1, axis)


WIDE = False


def mx_kscale(k):
    if not WIDE:
        return np.ones(k)
    levels = np.array([10, -10, 5, -5, 0])
    if k % 512:
        return np.exp2(np.random.permutation(np.resize(levels, k // 32))).repeat(32)
    a = np.empty((k // 512, 16))
    for p in range(k // 512):
        a[p, :8] = np.random.permutation(np.resize(levels, 8))
        for g in range(8):
            far = levels[np.abs(levels - a[p, g]) >= 10]
            a[p, g + 8] = far[np.random.randint(len(far))]
    return np.exp2(a.ravel()).repeat(32)


def f64(x):
    return np.asarray(x).astype(np.float64)


def striped(idx):
    return np.tile(idx.reshape(-1, 16).T, (8, 1)).astype(np.uint16)


def unstriped(offs):
    return offs[:16].T.reshape(-1).astype(np.int64)


E2M1 = np.array([0.0, 0.5, 1.0, 1.5, 2.0, 3.0, 4.0, 6.0, -0.0, -0.5, -1.0, -1.5, -2.0, -3.0, -4.0, -6.0])


def pack_weight(w, fmt):
    k, n = w.shape
    w = f64(np.asarray(w, np.float32).astype(ml_dtypes.bfloat16)).reshape(k // 32, 32, n)
    amax = np.abs(w).max(1)
    if fmt == "e4m3":
        byte = np.frexp(amax)[1] - 1 + 127 - 7
    else:
        mant, ex = np.frexp(amax / 6.0)
        byte = np.where(mant > 0.5, ex, ex - 1) + 127
    byte = np.clip(np.where(amax > 0, byte, 1), 1, 254)
    scaled = (w * np.exp2(127.0 - byte)[:, None, :]).reshape(k, n).astype(np.float32)
    by_word = np.ascontiguousarray(scaled.reshape(k // 512, 128, 4, n).transpose(0, 1, 3, 2))
    if fmt == "e4m3":
        words = by_word.astype(ml_dtypes.float8_e4m3fn).view(np.uint8)
    else:
        c = by_word.astype(ml_dtypes.float4_e2m1fn).view(np.uint8) & 0xF
        words = (c[..., 0::2] | (c[..., 1::2] << 4)).reshape(k // 512, 128, 2 * n)
    return np.ascontiguousarray(words), np.ascontiguousarray(byte.astype(np.uint8).reshape(k // 512, 16, n))


def unpack_weight(words, scales, fmt):
    g, _, n = scales.shape
    words = np.ascontiguousarray(words).reshape(g, 128, n, -1)
    if fmt == "e4m3":
        vals = words.view(ml_dtypes.float8_e4m3fn).astype(np.float64)
    else:
        nib = np.empty((g, 128, n, 4), np.uint8)
        nib[..., 0::2] = words & 0xF
        nib[..., 1::2] = words >> 4
        vals = E2M1[nib]
    vals = vals * np.repeat(np.exp2(scales.astype(np.float64) - 127.0), 8, axis=1)[..., None]
    return vals.transpose(0, 1, 3, 2).reshape(g * 512, n)


def relu(v):
    return np.maximum(v, 0.0)


K, T, E, C, H, N = 1536, 768, 4, 128, 512, 128


def by_expert(wq, xq):
    return np.concatenate([wq[e].T @ xq[:, e * C:(e + 1) * C] for e in range(E)], axis=1)


def setup_inputs():
    n = np.random.standard_normal
    s = mx_kscale(K)[:, None]
    u = mx_kscale(H)
    x = pack_weight(n((K, T)) * s, "e4m3")
    return {
        "x_words": x[0],
        "x_scales": x[1],
        "w1": (n((E + 1, K, H)) / np.sqrt(K) / s[None] * u[None, None, :]).astype(np.float32),
        "w2": (n((E + 1, H, N)) / np.sqrt(H) / u[None, :, None]).astype(np.float32),
        "gate": np.tile(np.random.uniform(0.2, 1.0, E * C), (N, 1)).astype(np.float32),
        "offs": striped(np.random.permutation(T)[:E * C]),
    }


def reference(x_words, x_scales, w1, w2, gate, offs):
    idx = unstriped(offs)
    w1q, w2q = mxq(f64(w1), 1, "e4m3"), mxq(f64(w2), 1, "e4m3")
    xs = unpack_weight(x_words, x_scales, "e4m3")
    hs = relu(w1q[E].T @ xs)
    ys = w2q[E].T @ mxq(hs, 0, "e4m3")
    xq = unpack_weight(x_words, x_scales, "e4m3")[:, idx]
    h = relu(by_expert(w1q, xq))
    y = by_expert(w2q, mxq(h, 0, "e4m3"))
    out = ys
    out[:, idx] += f64(gate) * y
    return out

@@ -1,0 +1,177 @@
+from contextlib import ExitStack
+
+import concourse.mybir as mybir
+
+K, T, E, C, H, N = 1536, 768, 4, 128, 512, 128
+FLOPS = 2 * (E * C + T) * (K * H + H * N)
+
+F32 = mybir.dt.float32
+BF16 = mybir.dt.bfloat16
+I32 = mybir.dt.int32
+U32 = mybir.dt.uint32
+U16 = mybir.dt.uint16
+U8 = mybir.dt.uint8
+FP8X4 = mybir.dt.float8_e4m3fn_x4
+COPY = mybir.ActivationFunctionType.Copy
+RELU = mybir.ActivationFunctionType.Relu
+MULT = mybir.AluOpType.mult
+ADD = mybir.AluOpType.add
+
+P = 128
+PACK = 4
+K_PASS = P * PACK
+PASSES = K // K_PASS
+S = E * C
+SHARED = E
+M_SCALAR = 64
+M_SCALAR_LAST = 44
+OUT_PIECE = 256
+
+
+def tile_moe_shr_mlp_relu_kernel(tc, x_words, x_scales, w1, w2, gate, offs, out):
+    nc = tc.nc
+    with ExitStack() as ctx:
+        keep = ctx.enter_context(tc.tile_pool(name="keep", bufs=1))
+        stage = ctx.enter_context(tc.tile_pool(name="stage", bufs=4))
+        codes = ctx.enter_context(tc.tile_pool(name="codes", bufs=6))
+        psum_h = ctx.enter_context(tc.psum_pool(name="psum_h", bufs=4))
+        psum_y = ctx.enter_context(tc.psum_pool(name="psum_y", bufs=2))
+        psum_s = ctx.enter_context(tc.psum_pool(name="psum_s", bufs=1))
+
+        offsets = keep.tile([P, S // 16], U16, name="offsets")
+        nc.sync.dma_start(offsets[:], offs)
+
+        xs = keep.tile([P, T], U8, name="xs", align_bytes=64)
+        nc.vector.memset(xs[:].bitcast(I32), 0)
+        for q in range(4):
+            nc.scalar.dma_start(
+                out=xs[32 * q : 32 * q + 4 * PASSES, :].bitcast(I32),
+                in_=x_scales[:, 4 * q : 4 * q + 4, :].bitcast(I32),
+            )
+
+        w1_raw = {}
+        w2_raw = {}
+        xw = []
+
+        def load_w1(e, o):
+            raw = keep.tile([P, PACK, H], F32, name="w1_raw_%d_%d" % (e, o))
+            nc.sync.dma_start(out=raw[:], in_=w1[e, o * K_PASS : (o + 1) * K_PASS, :].rearrange("(p j) c -> p j c", j=PACK))
+            w1_raw[(e, o)] = raw
+
+        def load_w2(e):
+            raw = keep.tile([P, PACK, N], F32, name="w2_raw_%d" % e)
+            nc.sync.dma_start(out=raw[:], in_=w2[e].rearrange("(p j) n -> p j n", j=PACK))
+            w2_raw[e] = raw
+
+        load_w1(SHARED, 0)
+        for o in range(PASSES):
+            words = keep.tile([P, T], U32, name="xw_%d" % o, align_bytes=64)
+            nc.sync.dma_start(out=words[:].bitcast(I32), in_=x_words[o].rearrange("p t r -> p (t r)").bitcast(I32))
+            xw.append(words)
+        for o in range(1, PASSES):
+            load_w1(SHARED, o)
+        gate_sb = keep.tile([P, S], F32, name="gate_sb")
+        for e in range(E):
+            for o in range(PASSES):
+                load_w1(e, o)
+            load_w2(e)
+            if e == 0:
+                nc.sync.dma_start(out=gate_sb[:], in_=gate)
+        load_w2(SHARED)
+
+        routed = keep.tile([P, T], F32, name="routed")
+        nc.vector.memset(routed[:], 0.0)
+
+        def quantise_w1(e, o, m_scalar):
+            grouped = stage.tile([P, PACK, P, PACK], BF16, name="w1_grouped", align_bytes=64)
+            dst = grouped[:].rearrange("p t m j -> p m j t")
+            src = w1_raw[(e, o)][:].rearrange("p j (m t) -> p m j t", t=PACK)
+            nc.scalar.activation(out=dst[:, 0:m_scalar], in_=src[:, 0:m_scalar], func=COPY)
+            nc.vector.tensor_copy(out=dst[:, m_scalar:P], in_=src[:, m_scalar:P])
+            wc = codes.tile([P, H], U32, name="w1_codes", align_bytes=64)
+            ws = codes.tile([P, H], U8, name="w1_scales", align_bytes=64)
+            nc.vector.quantize_mx(out=wc[:].bitcast(FP8X4), scales=ws[:], in_=grouped[:].rearrange("p t m j -> p (t m j)"))
+            return wc, ws
+
+        def quantise_w2(e):
+            grouped = stage.tile([P, N, PACK], BF16, name="w2_grouped", align_bytes=64)
+            nc.scalar.activation(
+                out=grouped[:].rearrange("p (c i) j -> p c j i", i=4),
+                in_=w2_raw[e][:].rearrange("p j (c i) -> p c j i", i=4),
+                func=COPY,
+            )
+            wc = keep.tile([P, N], U32, name="w2_codes_%d" % e, align_bytes=64)
+            ws = keep.tile([P, N], U8, name="w2_scales_%d" % e, align_bytes=64)
+            nc.vector.quantize_mx(out=wc[:].bitcast(FP8X4), scales=ws[:], in_=grouped[:].rearrange("p n j -> p (n j)"))
+            return wc, ws
+
+        def first_layer(w1q, words, scales, cols, hidden):
+            acc = psum_h.tile([P, PACK, C], F32, name="acc_h")
+            for t in range(PACK):
+                for o in range(PASSES):
+                    wc, ws = w1q[o]
+                    nc.tensor.matmul_mx(
+                        out=acc[:, t, :],
+                        lhsT=wc[:, t * P : (t + 1) * P].bitcast(FP8X4),
+                        lhsT_scale=ws[:, t * P : (t + 1) * P],
+                        rhs=words[o][:, cols].bitcast(FP8X4),
+                        rhs_scale=scales[4 * o : P, cols],
+                        start=(o == 0),
+                        stop=(o == PASSES - 1),
+                    )
+            nc.scalar.activation(out=hidden, in_=acc[:].rearrange("p t c -> p c t"), func=RELU)
+
+        w1q = [quantise_w1(SHARED, o, M_SCALAR) for o in range(PASSES)]
+
+        gw = []
+        for o in range(PASSES):
+            g = keep.tile([P, S], U32, name="gw_%d" % o, align_bytes=64)
+            nc.vector.tensor_copy(g[:], xw[o][:].indirect(offsets[:]))
+            gw.append(g)
+        gs = keep.tile([P, S], U8, name="gs", align_bytes=64)
+        nc.vector.tensor_copy(gs[:], xs[:].indirect(offsets[:]))
+
+        hs_codes = []
+        for piece in range(T // OUT_PIECE):
+            hidden = stage.tile([P, OUT_PIECE, PACK], BF16, name="hs_grouped", align_bytes=64)
+            for half in range(OUT_PIECE // C):
+                first = piece * OUT_PIECE + half * C
+                first_layer(w1q, xw, xs, slice(first, first + C), hidden[:, half * C : (half + 1) * C, :])
+            hc = keep.tile([P, OUT_PIECE], U32, name="hs_codes_%d" % piece, align_bytes=64)
+            hsc = keep.tile([P, OUT_PIECE], U8, name="hs_scales_%d" % piece, align_bytes=64)
+            nc.vector.quantize_mx(out=hc[:].bitcast(FP8X4), scales=hsc[:], in_=hidden[:].rearrange("p c t -> p (c t)"))
+            hs_codes.append((hc, hsc))
+
+        for e in range(E):
+            w1q = [quantise_w1(e, o, M_SCALAR_LAST if (e, o) == (E - 1, PASSES - 1) else M_SCALAR) for o in range(PASSES)]
+            slots = slice(e * C, (e + 1) * C)
+            hidden = stage.tile([P, C, PACK], BF16, name="h_grouped", align_bytes=64)
+            first_layer(w1q, gw, gs, slots, hidden[:])
+            w2c, w2s = quantise_w2(e)
+            hc = codes.tile([P, C], U32, name="h_codes", align_bytes=64)
+            hsc = codes.tile([P, C], U8, name="h_scales", align_bytes=64)
+            nc.vector.quantize_mx(out=hc[:].bitcast(FP8X4), scales=hsc[:], in_=hidden[:].rearrange("p c t -> p (c t)"))
+            acc_y = psum_y.tile([P, C], F32, name="acc_y")
+            nc.tensor.matmul_mx(
+                out=acc_y[:], lhsT=w2c[:].bitcast(FP8X4), lhsT_scale=w2s[:], rhs=hc[:].bitcast(FP8X4), rhs_scale=hsc[:],
+                start=True, stop=True,
+            )
+            y = stage.tile([P, C], F32, name="y")
+            nc.scalar.activation(out=y[:], in_=acc_y[:], func=COPY)
+            nc.vector.tensor_tensor(routed[:].indirect(offsets[:, e * C // 16 : (e + 1) * C // 16]), y[:], gate_sb[:, slots], MULT)
+
+        w2c, w2s = quantise_w2(SHARED)
+        acc_a = psum_s.tile([P, 2 * OUT_PIECE], F32, name="acc_a")
+        acc_b = psum_s.tile([P, OUT_PIECE], F32, name="acc_b")
+        accs = [acc_a[:, 0:OUT_PIECE], acc_a[:, OUT_PIECE : 2 * OUT_PIECE], acc_b[:]]
+        for piece in range(T // OUT_PIECE):
+            hc, hsc = hs_codes[piece]
+            nc.tensor.matmul_mx(
+                out=accs[piece], lhsT=w2c[:].bitcast(FP8X4), lhsT_scale=w2s[:], rhs=hc[:].bitcast(FP8X4), rhs_scale=hsc[:],
+                start=True, stop=True,
+            )
+        for piece in range(T // OUT_PIECE):
+            cols = slice(piece * OUT_PIECE, (piece + 1) * OUT_PIECE)
+            result = stage.tile([P, OUT_PIECE], F32, name="result")
+            nc.vector.tensor_tensor(result[:], routed[:, cols], accs[piece], ADD)
+            nc.sync.dma_start(out=out[:, cols], in_=result[:])

@@ -23,9 +23,9 @@ K_PASS = P * PACK
 PASSES = K // K_PASS
 S = E * C
 SHARED = E
-M_SCALAR = 64
-M_SCALAR_LAST = 44
+HALF = PACK // 2
 OUT_PIECE = 256
+GROUPS = T // C
 
 
 def tile_moe_shr_mlp_relu_kernel(tc, x_words, x_scales, w1, w2, gate, offs, out):
@@ -33,13 +33,10 @@ def tile_moe_shr_mlp_relu_kernel(tc, x_words, x_scales, w1, w2, gate, offs, out)
     with ExitStack() as ctx:
         keep = ctx.enter_context(tc.tile_pool(name="keep", bufs=1))
         stage = ctx.enter_context(tc.tile_pool(name="stage", bufs=4))
-        codes = ctx.enter_context(tc.tile_pool(name="codes", bufs=6))
+        codes = ctx.enter_context(tc.tile_pool(name="codes", bufs=16))
         psum_h = ctx.enter_context(tc.psum_pool(name="psum_h", bufs=4))
         psum_y = ctx.enter_context(tc.psum_pool(name="psum_y", bufs=2))
         psum_s = ctx.enter_context(tc.psum_pool(name="psum_s", bufs=1))
-
-        offsets = keep.tile([P, S // 16], U16, name="offsets")
-        nc.sync.dma_start(offsets[:], offs)
 
         xs = keep.tile([P, T], U8, name="xs", align_bytes=64)
         nc.vector.memset(xs[:].bitcast(I32), 0)
@@ -49,12 +46,19 @@ def tile_moe_shr_mlp_relu_kernel(tc, x_words, x_scales, w1, w2, gate, offs, out)
                 in_=x_scales[:, 4 * q : 4 * q + 4, :].bitcast(I32),
             )
 
+        routed = keep.tile([P, T], F32, name="routed")
+        nc.vector.memset(routed[:, 0 : T // 2], 0.0)
+        nc.scalar.activation(out=routed[:, T // 2 : T], in_=routed[:, 0 : T // 2], func=COPY)
+
         w1_raw = {}
         w2_raw = {}
         xw = []
 
+        def raw_tag(e, o):
+            return "w1_raw_%d_%d" % (e, o)
+
         def load_w1(e, o):
-            raw = keep.tile([P, PACK, H], F32, name="w1_raw_%d_%d" % (e, o))
+            raw = keep.tile([P, PACK, H], F32, name=raw_tag(e, o), tag=raw_tag(e, o), align_bytes=64)
             nc.sync.dma_start(out=raw[:], in_=w1[e, o * K_PASS : (o + 1) * K_PASS, :].rearrange("(p j) c -> p j c", j=PACK))
             w1_raw[(e, o)] = raw
 
@@ -64,34 +68,65 @@ def tile_moe_shr_mlp_relu_kernel(tc, x_words, x_scales, w1, w2, gate, offs, out)
             w2_raw[e] = raw
 
         load_w1(SHARED, 0)
+        offsets = keep.tile([P, S // 16], U16, name="offsets")
+        nc.sync.dma_start(offsets[:], offs)
         for o in range(PASSES):
             words = keep.tile([P, T], U32, name="xw_%d" % o, align_bytes=64)
             nc.sync.dma_start(out=words[:].bitcast(I32), in_=x_words[o].rearrange("p t r -> p (t r)").bitcast(I32))
             xw.append(words)
         for o in range(1, PASSES):
             load_w1(SHARED, o)
-        gate_sb = keep.tile([P, S], F32, name="gate_sb")
+        gates = [keep.tile([P, S // 2], F32, name="gate_%d" % i) for i in range(2)]
+        last_raw = [keep.tile([P, PACK, H // 2], F32, name="last_raw_%d" % i) for i in range(2)]
         for e in range(E):
             for o in range(PASSES):
-                load_w1(e, o)
-            load_w2(e)
+                if (e, o) != (E - 1, PASSES - 1):
+                    load_w1(e, o)
+            if e < E - 2:
+                load_w2(e)
             if e == 0:
-                nc.sync.dma_start(out=gate_sb[:], in_=gate)
+                nc.sync.dma_start(out=gates[0][:], in_=gate[:, 0 : S // 2])
+        last_rows = w1[E - 1, K - K_PASS : K, :].rearrange("(p j) c -> p j c", j=PACK)
+        for i in range(2):
+            nc.sync.dma_start(out=last_raw[i][:], in_=last_rows[:, :, i * H // 2 : (i + 1) * H // 2])
+        load_w2(E - 2)
+        nc.sync.dma_start(out=gates[1][:], in_=gate[:, S // 2 : S])
+        load_w2(E - 1)
         load_w2(SHARED)
 
-        routed = keep.tile([P, T], F32, name="routed")
-        nc.vector.memset(routed[:], 0.0)
-
-        def quantise_w1(e, o, m_scalar):
-            grouped = stage.tile([P, PACK, P, PACK], BF16, name="w1_grouped", align_bytes=64)
-            dst = grouped[:].rearrange("p t m j -> p m j t")
-            src = w1_raw[(e, o)][:].rearrange("p j (m t) -> p m j t", t=PACK)
-            nc.scalar.activation(out=dst[:, 0:m_scalar], in_=src[:, 0:m_scalar], func=COPY)
-            nc.vector.tensor_copy(out=dst[:, m_scalar:P], in_=src[:, m_scalar:P])
-            wc = codes.tile([P, H], U32, name="w1_codes", align_bytes=64)
-            ws = codes.tile([P, H], U8, name="w1_scales", align_bytes=64)
-            nc.vector.quantize_mx(out=wc[:].bitcast(FP8X4), scales=ws[:], in_=grouped[:].rearrange("p t m j -> p (t m j)"))
+        def quantise(grouped, width, name):
+            wc = codes.tile([P, width], U32, name=name + "_codes", align_bytes=64)
+            ws = codes.tile([P, width], U8, name=name + "_scales", align_bytes=64)
+            nc.vector.quantize_mx(out=wc[:].bitcast(FP8X4), scales=ws[:], in_=grouped)
             return wc, ws
+
+        def quantise_w1(e, o):
+            src = w1_raw[(e, o)][:].rearrange("p j (m t) -> p m j t", t=PACK)
+            low = stage.tile([P, HALF, P, PACK], BF16, name="w1_low", align_bytes=64)
+            high = stage.tile([P, HALF, P, PACK], BF16, name="w1_high", align_bytes=64)
+            nc.vector.tensor_copy(out=low[:].rearrange("p t m j -> p m j t"), in_=src[:, :, :, 0:HALF])
+            nc.scalar.activation(out=high[:].rearrange("p t m j -> p m j t"), in_=src[:, :, :, HALF:PACK], func=COPY)
+            return [quantise(half[:].rearrange("p t m j -> p (t m j)"), HALF * P, "w1") for half in (low, high)]
+
+        def quantise_last():
+            made = []
+            for half in range(2):
+                wc = codes.tile([P, HALF * P], U32, name="w1_codes", align_bytes=64)
+                ws = codes.tile([P, HALF * P], U8, name="w1_scales", align_bytes=64)
+                made.append((wc, ws))
+            for i in range(2):
+                src = last_raw[i][:].rearrange("p j (m t) -> p m j t", t=PACK)
+                low = stage.tile([P, HALF, P // 2, PACK], BF16, name="w1_low", align_bytes=64)
+                high = stage.tile([P, HALF, P // 2, PACK], BF16, name="w1_high", align_bytes=64)
+                nc.vector.tensor_copy(out=low[:].rearrange("p t m j -> p m j t"), in_=src[:, :, :, 0:HALF])
+                nc.scalar.activation(out=high[:].rearrange("p t m j -> p m j t"), in_=src[:, :, :, HALF:PACK], func=COPY)
+                for (wc, ws), half in zip(made, (low, high)):
+                    for t in range(HALF):
+                        cols = slice(t * P + i * P // 2, t * P + (i + 1) * P // 2)
+                        nc.vector.quantize_mx(
+                            out=wc[:, cols].bitcast(FP8X4), scales=ws[:, cols], in_=half[:, t].rearrange("p m j -> p (m j)")
+                        )
+            return made
 
         def quantise_w2(e):
             grouped = stage.tile([P, N, PACK], BF16, name="w2_grouped", align_bytes=64)
@@ -100,75 +135,102 @@ def tile_moe_shr_mlp_relu_kernel(tc, x_words, x_scales, w1, w2, gate, offs, out)
                 in_=w2_raw[e][:].rearrange("p j (c i) -> p c j i", i=4),
                 func=COPY,
             )
-            wc = keep.tile([P, N], U32, name="w2_codes_%d" % e, align_bytes=64)
-            ws = keep.tile([P, N], U8, name="w2_scales_%d" % e, align_bytes=64)
-            nc.vector.quantize_mx(out=wc[:].bitcast(FP8X4), scales=ws[:], in_=grouped[:].rearrange("p n j -> p (n j)"))
-            return wc, ws
+            return quantise(grouped[:].rearrange("p n j -> p (n j)"), N, "w2")
 
-        def first_layer(w1q, words, scales, cols, hidden):
+        def first_layer(w1q, words, scales, cols):
             acc = psum_h.tile([P, PACK, C], F32, name="acc_h")
             for t in range(PACK):
                 for o in range(PASSES):
-                    wc, ws = w1q[o]
+                    wc, ws = w1q[o][t // HALF]
+                    part = slice((t % HALF) * P, (t % HALF + 1) * P)
                     nc.tensor.matmul_mx(
                         out=acc[:, t, :],
-                        lhsT=wc[:, t * P : (t + 1) * P].bitcast(FP8X4),
-                        lhsT_scale=ws[:, t * P : (t + 1) * P],
+                        lhsT=wc[:, part].bitcast(FP8X4),
+                        lhsT_scale=ws[:, part],
                         rhs=words[o][:, cols].bitcast(FP8X4),
                         rhs_scale=scales[4 * o : P, cols],
                         start=(o == 0),
                         stop=(o == PASSES - 1),
                     )
+            return acc
+
+        def relu_out(acc, hidden):
             nc.scalar.activation(out=hidden, in_=acc[:].rearrange("p t c -> p c t"), func=RELU)
 
-        w1q = [quantise_w1(SHARED, o, M_SCALAR) for o in range(PASSES)]
+        w1q_shared = [quantise_w1(SHARED, o) for o in range(PASSES)]
 
         gw = []
         for o in range(PASSES):
-            g = keep.tile([P, S], U32, name="gw_%d" % o, align_bytes=64)
+            tag = raw_tag(SHARED, 1) if o == PASSES - 1 else "gw_%d" % o
+            g = keep.tile([P, S], U32, name="gw_%d" % o, tag=tag, align_bytes=64)
             nc.vector.tensor_copy(g[:], xw[o][:].indirect(offsets[:]))
             gw.append(g)
-        gs = keep.tile([P, S], U8, name="gs", align_bytes=64)
+        gs = keep.tile([P, S], U8, name="gs", tag=raw_tag(SHARED, 2), align_bytes=64)
         nc.vector.tensor_copy(gs[:], xs[:].indirect(offsets[:]))
 
-        hs_codes = []
-        for piece in range(T // OUT_PIECE):
-            hidden = stage.tile([P, OUT_PIECE, PACK], BF16, name="hs_grouped", align_bytes=64)
-            for half in range(OUT_PIECE // C):
-                first = piece * OUT_PIECE + half * C
-                first_layer(w1q, xw, xs, slice(first, first + C), hidden[:, half * C : (half + 1) * C, :])
-            hc = keep.tile([P, OUT_PIECE], U32, name="hs_codes_%d" % piece, align_bytes=64)
-            hsc = keep.tile([P, OUT_PIECE], U8, name="hs_scales_%d" % piece, align_bytes=64)
-            nc.vector.quantize_mx(out=hc[:].bitcast(FP8X4), scales=hsc[:], in_=hidden[:].rearrange("p c t -> p (c t)"))
-            hs_codes.append((hc, hsc))
+        hs_codes = keep.tile([P, T], U32, name="hs_codes", align_bytes=64)
+        hs_scales = keep.tile([P, T], U8, name="hs_scales", align_bytes=64)
 
-        for e in range(E):
-            w1q = [quantise_w1(e, o, M_SCALAR_LAST if (e, o) == (E - 1, PASSES - 1) else M_SCALAR) for o in range(PASSES)]
-            slots = slice(e * C, (e + 1) * C)
-            hidden = stage.tile([P, C, PACK], BF16, name="h_grouped", align_bytes=64)
-            first_layer(w1q, gw, gs, slots, hidden[:])
-            w2c, w2s = quantise_w2(e)
-            hc = codes.tile([P, C], U32, name="h_codes", align_bytes=64)
-            hsc = codes.tile([P, C], U8, name="h_scales", align_bytes=64)
-            nc.vector.quantize_mx(out=hc[:].bitcast(FP8X4), scales=hsc[:], in_=hidden[:].rearrange("p c t -> p (c t)"))
+        def shared_group(group, hidden):
+            cols = slice(group * C, (group + 1) * C)
+            relu_out(first_layer(w1q_shared, xw, xs, cols), hidden)
+            nc.vector.quantize_mx(
+                out=hs_codes[:, cols].bitcast(FP8X4), scales=hs_scales[:, cols], in_=hidden.rearrange("p c t -> p (c t)")
+            )
+
+        def routed_hidden(e, w1q, hidden):
+            relu_out(first_layer(w1q, gw, gs, slice(e * C, (e + 1) * C)), hidden)
+            return quantise(hidden.rearrange("p c t -> p (c t)"), C, "h")
+
+        def second_layer(e, w2q, hq, y):
             acc_y = psum_y.tile([P, C], F32, name="acc_y")
             nc.tensor.matmul_mx(
-                out=acc_y[:], lhsT=w2c[:].bitcast(FP8X4), lhsT_scale=w2s[:], rhs=hc[:].bitcast(FP8X4), rhs_scale=hsc[:],
+                out=acc_y[:], lhsT=w2q[0][:].bitcast(FP8X4), lhsT_scale=w2q[1][:], rhs=hq[0][:].bitcast(FP8X4), rhs_scale=hq[1][:],
                 start=True, stop=True,
             )
-            y = stage.tile([P, C], F32, name="y")
             nc.scalar.activation(out=y[:], in_=acc_y[:], func=COPY)
-            nc.vector.tensor_tensor(routed[:].indirect(offsets[:, e * C // 16 : (e + 1) * C // 16]), y[:], gate_sb[:, slots], MULT)
+            nc.vector.tensor_tensor(
+                routed[:].indirect(offsets[:, e * C // 16 : (e + 1) * C // 16]), y[:],
+                gates[e // 2][:, (e % 2) * C : (e % 2 + 1) * C], MULT
+            )
+
+        previous = None
+        hq = None
+        group = 0
+        for e in range(E):
+            w1q = []
+            for o in range(PASSES):
+                w1q.append(quantise_w1(e, o) if (e, o) != (E - 1, PASSES - 1) else quantise_last())
+                step = e * PASSES + o
+                if step <= PASSES or o == 0:
+                    hidden = keep.tile([P, 2, C, PACK], BF16, name="hidden_%d" % step, tag=raw_tag(e, o), align_bytes=64)
+                    if step <= PASSES:
+                        shared_group(group, hidden[:, 0])
+                        group = group + 1
+                    if 0 < step < PASSES:
+                        shared_group(group, hidden[:, 1])
+                        group = group + 1
+                    if e > 0:
+                        hq = routed_hidden(e - 1, previous[0], hidden[:, 1])
+                elif o == 1 and e < E - 1:
+                    y = keep.tile([P, C], F32, name="y_%d" % e, tag=raw_tag(e, o), align_bytes=64)
+                    second_layer(e - 1, previous[1], hq, y)
+            previous = (w1q, quantise_w2(e) if e < E - 2 else None)
+        y_before = keep.tile([P, C], F32, name="y_before")
+        second_layer(E - 2, quantise_w2(E - 2), hq, y_before)
+        hidden = keep.tile([P, C, PACK], BF16, name="hidden_last", align_bytes=64)
+        y = keep.tile([P, C], F32, name="y_last")
+        second_layer(E - 1, quantise_w2(E - 1), routed_hidden(E - 1, previous[0], hidden[:]), y)
 
         w2c, w2s = quantise_w2(SHARED)
         acc_a = psum_s.tile([P, 2 * OUT_PIECE], F32, name="acc_a")
         acc_b = psum_s.tile([P, OUT_PIECE], F32, name="acc_b")
         accs = [acc_a[:, 0:OUT_PIECE], acc_a[:, OUT_PIECE : 2 * OUT_PIECE], acc_b[:]]
         for piece in range(T // OUT_PIECE):
-            hc, hsc = hs_codes[piece]
+            cols = slice(piece * OUT_PIECE, (piece + 1) * OUT_PIECE)
             nc.tensor.matmul_mx(
-                out=accs[piece], lhsT=w2c[:].bitcast(FP8X4), lhsT_scale=w2s[:], rhs=hc[:].bitcast(FP8X4), rhs_scale=hsc[:],
-                start=True, stop=True,
+                out=accs[piece], lhsT=w2c[:].bitcast(FP8X4), lhsT_scale=w2s[:], rhs=hs_codes[:, cols].bitcast(FP8X4),
+                rhs_scale=hs_scales[:, cols], start=True, stop=True,
             )
         for piece in range(T // OUT_PIECE):
             cols = slice(piece * OUT_PIECE, (piece + 1) * OUT_PIECE)

@@ -1,6 +1,7 @@
 from contextlib import ExitStack
 
 import concourse.mybir as mybir
+from concourse.masks import make_identity
 
 K, T, E, C, H, N = 1536, 768, 4, 128, 512, 128
 FLOPS = 2 * (E * C + T) * (K * H + H * N)
@@ -21,11 +22,17 @@ P = 128
 PACK = 4
 K_PASS = P * PACK
 PASSES = K // K_PASS
-S = E * C
+SLOTS = E * C
 SHARED = E
-HALF = PACK // 2
-OUT_PIECE = 256
+LAST = E - 1
+PAIR = PACK // 2
+QUADRANT = 32
+SCALE_ROWS = 4
+OFFSETS_PER_COLUMN = 16
+RUN = 4
 GROUPS = T // C
+OUT_PIECE = 256
+ALIGN = 64
 
 
 def tile_moe_shr_mlp_relu_kernel(tc, x_words, x_scales, w1, w2, gate, offs, out):
@@ -33,207 +40,244 @@ def tile_moe_shr_mlp_relu_kernel(tc, x_words, x_scales, w1, w2, gate, offs, out)
     with ExitStack() as ctx:
         keep = ctx.enter_context(tc.tile_pool(name="keep", bufs=1))
         stage = ctx.enter_context(tc.tile_pool(name="stage", bufs=4))
-        codes = ctx.enter_context(tc.tile_pool(name="codes", bufs=16))
-        psum_h = ctx.enter_context(tc.psum_pool(name="psum_h", bufs=4))
+        codes = ctx.enter_context(tc.tile_pool(name="codes", bufs=1))
+        psum_h = ctx.enter_context(tc.psum_pool(name="psum_h", bufs=2))
         psum_y = ctx.enter_context(tc.psum_pool(name="psum_y", bufs=2))
         psum_s = ctx.enter_context(tc.psum_pool(name="psum_s", bufs=1))
 
-        xs = keep.tile([P, T], U8, name="xs", align_bytes=64)
-        nc.vector.memset(xs[:].bitcast(I32), 0)
-        for q in range(4):
+        x_scale_tile = keep.tile([P, T], U8, name="x_scale_tile", align_bytes=ALIGN)
+        nc.gpsimd.memset(x_scale_tile[:].bitcast(I32), 0)
+        for q in range(P // QUADRANT):
             nc.scalar.dma_start(
-                out=xs[32 * q : 32 * q + 4 * PASSES, :].bitcast(I32),
-                in_=x_scales[:, 4 * q : 4 * q + 4, :].bitcast(I32),
+                out=x_scale_tile[QUADRANT * q : QUADRANT * q + SCALE_ROWS * PASSES, :].bitcast(I32),
+                in_=x_scales[:, SCALE_ROWS * q : SCALE_ROWS * (q + 1), :].bitcast(I32),
             )
 
+        gate_rows = keep.tile([P, C], F32, name="gate_rows")
+        nc.gpsimd.memset(gate_rows[:], 0.0)
+        nc.scalar.dma_start(out=gate_rows[0:E, :], in_=gate[0, :].rearrange("(e c) -> e c", e=E))
+        identity = keep.tile([P, P], F32, name="identity")
+        make_identity(nc, identity[:])
+
         routed = keep.tile([P, T], F32, name="routed")
-        nc.vector.memset(routed[:, 0 : T // 2], 0.0)
-        nc.scalar.activation(out=routed[:, T // 2 : T], in_=routed[:, 0 : T // 2], func=COPY)
+        nc.vector.memset(routed[:], 0.0)
 
         w1_raw = {}
         w2_raw = {}
-        xw = []
 
-        def raw_tag(e, o):
+        def w1_tag(e, o):
             return "w1_raw_%d_%d" % (e, o)
 
+        def w2_tag(e):
+            return "w2_raw_%d" % e
+
+        def w1_rows(e, o):
+            return w1[e, o * K_PASS : (o + 1) * K_PASS, :].rearrange("(p j) c -> p j c", j=PACK)
+
         def load_w1(e, o):
-            raw = keep.tile([P, PACK, H], F32, name=raw_tag(e, o), tag=raw_tag(e, o), align_bytes=64)
-            nc.sync.dma_start(out=raw[:], in_=w1[e, o * K_PASS : (o + 1) * K_PASS, :].rearrange("(p j) c -> p j c", j=PACK))
-            w1_raw[(e, o)] = raw
+            w1_raw[(e, o)] = keep.tile([P, PACK, H], F32, name=w1_tag(e, o), tag=w1_tag(e, o), align_bytes=ALIGN)
+            nc.sync.dma_start(out=w1_raw[(e, o)][:], in_=w1_rows(e, o))
 
         def load_w2(e):
-            raw = keep.tile([P, PACK, N], F32, name="w2_raw_%d" % e)
-            nc.sync.dma_start(out=raw[:], in_=w2[e].rearrange("(p j) n -> p j n", j=PACK))
-            w2_raw[e] = raw
+            w2_raw[e] = keep.tile([P, PACK, N], F32, name=w2_tag(e), tag=w2_tag(e), align_bytes=ALIGN)
+            nc.sync.dma_start(out=w2_raw[e][:], in_=w2[e].rearrange("(p j) n -> p j n", j=PACK))
 
         load_w1(SHARED, 0)
-        offsets = keep.tile([P, S // 16], U16, name="offsets")
+        offsets = keep.tile([P, SLOTS // OFFSETS_PER_COLUMN], U16, name="offsets")
         nc.sync.dma_start(offsets[:], offs)
-        for o in range(PASSES):
-            words = keep.tile([P, T], U32, name="xw_%d" % o, align_bytes=64)
-            nc.sync.dma_start(out=words[:].bitcast(I32), in_=x_words[o].rearrange("p t r -> p (t r)").bitcast(I32))
-            xw.append(words)
+        x_word_tile = keep.tile([P, PASSES, T], U32, name="x_word_tile", align_bytes=ALIGN)
+        nc.sync.dma_start(out=x_word_tile[:].bitcast(I32), in_=x_words.rearrange("o p t r -> p o (t r)").bitcast(I32))
+        token_words = [x_word_tile[:, o, :] for o in range(PASSES)]
         for o in range(1, PASSES):
             load_w1(SHARED, o)
-        gates = [keep.tile([P, S // 2], F32, name="gate_%d" % i) for i in range(2)]
-        last_raw = [keep.tile([P, PACK, H // 2], F32, name="last_raw_%d" % i) for i in range(2)]
-        for e in range(E):
+        for e in range(LAST):
             for o in range(PASSES):
-                if (e, o) != (E - 1, PASSES - 1):
-                    load_w1(e, o)
-            if e < E - 2:
-                load_w2(e)
-            if e == 0:
-                nc.sync.dma_start(out=gates[0][:], in_=gate[:, 0 : S // 2])
-        last_rows = w1[E - 1, K - K_PASS : K, :].rearrange("(p j) c -> p j c", j=PACK)
-        for i in range(2):
-            nc.sync.dma_start(out=last_raw[i][:], in_=last_rows[:, :, i * H // 2 : (i + 1) * H // 2])
-        load_w2(E - 2)
-        nc.sync.dma_start(out=gates[1][:], in_=gate[:, S // 2 : S])
-        load_w2(E - 1)
+                load_w1(e, o)
+            load_w2(e)
+        for o in range(PASSES - 1):
+            load_w1(LAST, o)
+        final_raw = []
+        for half in range(2):
+            raw = keep.tile([P, PACK, H // 2], F32, name="final_raw_%d" % half, tag="final_raw_%d" % half, align_bytes=ALIGN)
+            nc.sync.dma_start(out=raw[:], in_=w1_rows(LAST, PASSES - 1)[:, :, half * H // 2 : (half + 1) * H // 2])
+            final_raw.append(raw)
+        load_w2(LAST)
         load_w2(SHARED)
 
-        def quantise(grouped, width, name):
-            wc = codes.tile([P, width], U32, name=name + "_codes", align_bytes=64)
-            ws = codes.tile([P, width], U8, name=name + "_scales", align_bytes=64)
-            nc.vector.quantize_mx(out=wc[:].bitcast(FP8X4), scales=ws[:], in_=grouped)
-            return wc, ws
+        def quantise(values, width, name, bufs):
+            words = codes.tile([P, width], U32, name=name + "_words", align_bytes=ALIGN, bufs=bufs)
+            scales = codes.tile([P, width], U8, name=name + "_scales", align_bytes=ALIGN, bufs=bufs)
+            nc.vector.quantize_mx(out=words[:].bitcast(FP8X4), scales=scales[:], in_=values)
+            return words, scales
+
+        def cast_planes(raw, lower, upper, scalar_alone):
+            source = raw[:].rearrange("p j (m t) -> p m j t", t=PACK)
+            lower_view = lower[:].rearrange("p t m j -> p m j t")
+            if scalar_alone:
+                nc.scalar.activation(out=lower_view, in_=source[:, :, :, 0:PAIR], func=COPY)
+            else:
+                nc.vector.tensor_copy(out=lower_view, in_=source[:, :, :, 0:PAIR])
+            nc.scalar.activation(out=upper[:].rearrange("p t m j -> p m j t"), in_=source[:, :, :, PAIR:PACK], func=COPY)
 
         def quantise_w1(e, o):
-            src = w1_raw[(e, o)][:].rearrange("p j (m t) -> p m j t", t=PACK)
-            low = stage.tile([P, HALF, P, PACK], BF16, name="w1_low", align_bytes=64)
-            high = stage.tile([P, HALF, P, PACK], BF16, name="w1_high", align_bytes=64)
-            nc.vector.tensor_copy(out=low[:].rearrange("p t m j -> p m j t"), in_=src[:, :, :, 0:HALF])
-            nc.scalar.activation(out=high[:].rearrange("p t m j -> p m j t"), in_=src[:, :, :, HALF:PACK], func=COPY)
-            return [quantise(half[:].rearrange("p t m j -> p (t m j)"), HALF * P, "w1") for half in (low, high)]
+            lower = stage.tile([P, PAIR, P, PACK], BF16, name="w1_lower", align_bytes=ALIGN)
+            upper = stage.tile([P, PAIR, P, PACK], BF16, name="w1_upper", align_bytes=ALIGN)
+            cast_planes(w1_raw[(e, o)], lower, upper, (e, o) == (SHARED, 1))
+            name, bufs = ("w1_shared", 2 * PASSES) if e == SHARED else ("w1_routed", 4 * PASSES)
+            return [quantise(pair[:].rearrange("p t m j -> p (t m j)"), PAIR * P, name, bufs) for pair in (lower, upper)]
 
-        def quantise_last():
+        def quantise_final_pass():
             made = []
+            for pair in range(2):
+                words = keep.tile([P, PAIR * P], U32, name="final_words_%d" % pair, tag="final_words_%d" % pair, align_bytes=ALIGN)
+                scales = keep.tile([P, PAIR * P], U8, name="final_scales_%d" % pair, align_bytes=ALIGN)
+                made.append((words, scales))
             for half in range(2):
-                wc = codes.tile([P, HALF * P], U32, name="w1_codes", align_bytes=64)
-                ws = codes.tile([P, HALF * P], U8, name="w1_scales", align_bytes=64)
-                made.append((wc, ws))
-            for i in range(2):
-                src = last_raw[i][:].rearrange("p j (m t) -> p m j t", t=PACK)
-                low = stage.tile([P, HALF, P // 2, PACK], BF16, name="w1_low", align_bytes=64)
-                high = stage.tile([P, HALF, P // 2, PACK], BF16, name="w1_high", align_bytes=64)
-                nc.vector.tensor_copy(out=low[:].rearrange("p t m j -> p m j t"), in_=src[:, :, :, 0:HALF])
-                nc.scalar.activation(out=high[:].rearrange("p t m j -> p m j t"), in_=src[:, :, :, HALF:PACK], func=COPY)
-                for (wc, ws), half in zip(made, (low, high)):
-                    for t in range(HALF):
-                        cols = slice(t * P + i * P // 2, t * P + (i + 1) * P // 2)
+                lower = keep.tile([P, PAIR, P // 2, PACK], BF16, name="final_lower_%d" % half, align_bytes=ALIGN)
+                upper = keep.tile([P, PAIR, P // 2, PACK], BF16, name="final_upper_%d" % half, align_bytes=ALIGN)
+                cast_planes(final_raw[half], lower, upper, False)
+                for (words, scales), pair in zip(made, (lower, upper)):
+                    for t in range(PAIR):
+                        cols = slice(t * P + half * P // 2, t * P + (half + 1) * P // 2)
                         nc.vector.quantize_mx(
-                            out=wc[:, cols].bitcast(FP8X4), scales=ws[:, cols], in_=half[:, t].rearrange("p m j -> p (m j)")
+                            out=words[:, cols].bitcast(FP8X4), scales=scales[:, cols], in_=pair[:, t].rearrange("p m j -> p (m j)")
                         )
             return made
 
-        def quantise_w2(e):
-            grouped = stage.tile([P, N, PACK], BF16, name="w2_grouped", align_bytes=64)
+        def quantise_w2(e, tag):
+            grouped = keep.tile([P, N, PACK], BF16, name="w2_grouped_%d" % e, tag=tag, align_bytes=ALIGN)
             nc.scalar.activation(
-                out=grouped[:].rearrange("p (c i) j -> p c j i", i=4),
-                in_=w2_raw[e][:].rearrange("p j (c i) -> p c j i", i=4),
+                out=grouped[:].rearrange("p (c i) j -> p c j i", i=RUN),
+                in_=w2_raw[e][:].rearrange("p j (c i) -> p c j i", i=RUN),
                 func=COPY,
             )
-            return quantise(grouped[:].rearrange("p n j -> p (n j)"), N, "w2")
+            return quantise(grouped[:].rearrange("p n j -> p (n j)"), N, "w2", E + 1)
 
-        def first_layer(w1q, words, scales, cols):
-            acc = psum_h.tile([P, PACK, C], F32, name="acc_h")
+        def first_layer_pass(acc, w1q, words, scales, cols, t, o):
+            w_words, w_scales = w1q[o][t // PAIR]
+            plane = slice((t % PAIR) * P, (t % PAIR + 1) * P)
+            nc.tensor.matmul_mx(
+                out=acc,
+                lhsT=w_words[:, plane].bitcast(FP8X4),
+                lhsT_scale=w_scales[:, plane],
+                rhs=words[o][:, cols].bitcast(FP8X4),
+                rhs_scale=scales[SCALE_ROWS * o : P, cols],
+                start=(o == 0),
+                stop=(o == PASSES - 1),
+            )
+
+        def first_layer(w1q, words, scales, cols, bank, hidden):
+            acc = psum_h.tile([P, PACK, C], F32, name=bank, tag=bank)
             for t in range(PACK):
                 for o in range(PASSES):
-                    wc, ws = w1q[o][t // HALF]
-                    part = slice((t % HALF) * P, (t % HALF + 1) * P)
-                    nc.tensor.matmul_mx(
-                        out=acc[:, t, :],
-                        lhsT=wc[:, part].bitcast(FP8X4),
-                        lhsT_scale=ws[:, part],
-                        rhs=words[o][:, cols].bitcast(FP8X4),
-                        rhs_scale=scales[4 * o : P, cols],
-                        start=(o == 0),
-                        stop=(o == PASSES - 1),
-                    )
-            return acc
-
-        def relu_out(acc, hidden):
+                    first_layer_pass(acc[:, t, :], w1q, words, scales, cols, t, o)
             nc.scalar.activation(out=hidden, in_=acc[:].rearrange("p t c -> p c t"), func=RELU)
 
-        w1q_shared = [quantise_w1(SHARED, o) for o in range(PASSES)]
+        def quantise_hidden(hidden):
+            return quantise(hidden.rearrange("p c t -> p (c t)"), C, "h", E)
 
-        gw = []
-        for o in range(PASSES):
-            tag = raw_tag(SHARED, 1) if o == PASSES - 1 else "gw_%d" % o
-            g = keep.tile([P, S], U32, name="gw_%d" % o, tag=tag, align_bytes=64)
-            nc.vector.tensor_copy(g[:], xw[o][:].indirect(offsets[:]))
-            gw.append(g)
-        gs = keep.tile([P, S], U8, name="gs", tag=raw_tag(SHARED, 2), align_bytes=64)
-        nc.vector.tensor_copy(gs[:], xs[:].indirect(offsets[:]))
-
-        hs_codes = keep.tile([P, T], U32, name="hs_codes", align_bytes=64)
-        hs_scales = keep.tile([P, T], U8, name="hs_scales", align_bytes=64)
-
-        def shared_group(group, hidden):
-            cols = slice(group * C, (group + 1) * C)
-            relu_out(first_layer(w1q_shared, xw, xs, cols), hidden)
-            nc.vector.quantize_mx(
-                out=hs_codes[:, cols].bitcast(FP8X4), scales=hs_scales[:, cols], in_=hidden.rearrange("p c t -> p (c t)")
-            )
-
-        def routed_hidden(e, w1q, hidden):
-            relu_out(first_layer(w1q, gw, gs, slice(e * C, (e + 1) * C)), hidden)
-            return quantise(hidden.rearrange("p c t -> p (c t)"), C, "h")
-
-        def second_layer(e, w2q, hq, y):
+        def second_layer(e, w2q, hq, y, gate_tile):
             acc_y = psum_y.tile([P, C], F32, name="acc_y")
             nc.tensor.matmul_mx(
-                out=acc_y[:], lhsT=w2q[0][:].bitcast(FP8X4), lhsT_scale=w2q[1][:], rhs=hq[0][:].bitcast(FP8X4), rhs_scale=hq[1][:],
-                start=True, stop=True,
+                out=acc_y[:],
+                lhsT=w2q[0][:].bitcast(FP8X4),
+                lhsT_scale=w2q[1][:],
+                rhs=hq[0][:].bitcast(FP8X4),
+                rhs_scale=hq[1][:],
+                start=True,
+                stop=True,
             )
-            nc.scalar.activation(out=y[:], in_=acc_y[:], func=COPY)
-            nc.vector.tensor_tensor(
-                routed[:].indirect(offsets[:, e * C // 16 : (e + 1) * C // 16]), y[:],
-                gates[e // 2][:, (e % 2) * C : (e % 2 + 1) * C], MULT
-            )
+            nc.scalar.activation(out=y, in_=acc_y[:], func=COPY)
+            entries = offsets[:, e * C // OFFSETS_PER_COLUMN : (e + 1) * C // OFFSETS_PER_COLUMN]
+            nc.vector.tensor_tensor(routed[:].indirect(entries), y, gate_tile[:, e * C : (e + 1) * C], MULT)
 
-        previous = None
-        hq = None
+        w1q_shared = [quantise_w1(SHARED, o) for o in range(PASSES)]
+        slot_words = []
+        for o in range(PASSES):
+            gathered = keep.tile([P, SLOTS], U32, name="slot_words_%d" % o, align_bytes=ALIGN)
+            nc.vector.tensor_copy(gathered[:], token_words[o].indirect(offsets[:]))
+            slot_words.append(gathered)
+        slot_scales = keep.tile([P, SLOTS], U8, name="slot_scales", tag=w1_tag(SHARED, PASSES - 1), align_bytes=ALIGN)
+        nc.vector.tensor_copy(slot_scales[:], x_scale_tile[:].indirect(offsets[:]))
+
+        gate_turned = psum_s.tile([P, P], F32, name="gate_turned", tag="ys_tail")
+        nc.tensor.transpose(gate_turned[:], gate_rows[:], identity[:])
+        gate_columns = keep.tile([P, E], F32, name="gate_columns", tag=w1_tag(SHARED, 1), align_bytes=ALIGN)
+        nc.scalar.copy(gate_columns[:], gate_turned[:, 0:E])
+        gate_spread = psum_s.tile([P, SLOTS], F32, name="gate_spread", tag="ys_head")
+        for e in range(E):
+            nc.tensor.transpose(gate_spread[:, e * C : (e + 1) * C], gate_columns[:, e : e + 1].to_broadcast([P, P]), identity[:])
+
+        hs_words = keep.tile([P, T], U32, name="hs_words", align_bytes=ALIGN)
+        hs_scales = keep.tile([P, T], U8, name="hs_scales", align_bytes=ALIGN)
+        w1q = {}
+        w2q = {}
+        hq = {}
+        gate_tile = None
         group = 0
         for e in range(E):
-            w1q = []
+            w1q[e] = []
             for o in range(PASSES):
-                w1q.append(quantise_w1(e, o) if (e, o) != (E - 1, PASSES - 1) else quantise_last())
-                step = e * PASSES + o
-                if step <= PASSES or o == 0:
-                    hidden = keep.tile([P, 2, C, PACK], BF16, name="hidden_%d" % step, tag=raw_tag(e, o), align_bytes=64)
-                    if step <= PASSES:
-                        shared_group(group, hidden[:, 0])
-                        group = group + 1
-                    if 0 < step < PASSES:
-                        shared_group(group, hidden[:, 1])
-                        group = group + 1
-                    if e > 0:
-                        hq = routed_hidden(e - 1, previous[0], hidden[:, 1])
-                elif o == 1 and e < E - 1:
-                    y = keep.tile([P, C], F32, name="y_%d" % e, tag=raw_tag(e, o), align_bytes=64)
-                    second_layer(e - 1, previous[1], hq, y)
-            previous = (w1q, quantise_w2(e) if e < E - 2 else None)
-        y_before = keep.tile([P, C], F32, name="y_before")
-        second_layer(E - 2, quantise_w2(E - 2), hq, y_before)
-        hidden = keep.tile([P, C, PACK], BF16, name="hidden_last", align_bytes=64)
-        y = keep.tile([P, C], F32, name="y_last")
-        second_layer(E - 1, quantise_w2(E - 1), routed_hidden(E - 1, previous[0], hidden[:]), y)
+                w1q[e].append(quantise_final_pass() if (e, o) == (LAST, PASSES - 1) else quantise_w1(e, o))
+                if o > 0 and group == GROUPS:
+                    continue
+                work = keep.tile([P, 2 * PACK * C], BF16, name="work_%d_%d" % (e, o), tag=w1_tag(e, o), align_bytes=ALIGN)
+                hidden = work[:, 0 : PACK * C].rearrange("p (c t) -> p c t", t=PACK)
+                if e > 0 and o == 0:
+                    first_layer(w1q[e - 1], slot_words, slot_scales, slice((e - 1) * C, e * C), "acc_routed", hidden)
+                    hq[e - 1] = quantise_hidden(hidden)
+                    continue
+                if e > 0 and o == 1:
+                    second_layer(e - 1, w2q[e - 1], hq[e - 1], work[:, PACK * C : (PACK + 2) * C].bitcast(F32), gate_tile)
+                tokens = slice(group * C, (group + 1) * C)
+                first_layer(w1q_shared, token_words, x_scale_tile, tokens, "acc_shared", hidden)
+                nc.vector.quantize_mx(
+                    out=hs_words[:, tokens].bitcast(FP8X4), scales=hs_scales[:, tokens], in_=hidden.rearrange("p c t -> p (c t)")
+                )
+                group = group + 1
+            if e < LAST:
+                w2q[e] = quantise_w2(e, "w2_grouped_%d" % e)
+            if e == 0:
+                gate_tile = keep.tile([P, SLOTS], F32, name="gate_tile", tag=w2_tag(0), align_bytes=ALIGN)
+                nc.scalar.copy(gate_tile[:], gate_spread[:])
 
-        w2c, w2s = quantise_w2(SHARED)
-        acc_a = psum_s.tile([P, 2 * OUT_PIECE], F32, name="acc_a")
-        acc_b = psum_s.tile([P, OUT_PIECE], F32, name="acc_b")
-        accs = [acc_a[:, 0:OUT_PIECE], acc_a[:, OUT_PIECE : 2 * OUT_PIECE], acc_b[:]]
+        y_before = keep.tile([P, C], F32, name="y_before", tag="final_raw_1", align_bytes=ALIGN)
+        second_layer(LAST - 1, w2q[LAST - 1], hq[LAST - 1], y_before[:], gate_tile)
+
+        acc_last = [
+            psum_h.tile([P, C], F32, name="acc_last_%d" % t, tag="acc_shared" if t < PAIR else "acc_routed") for t in range(PACK)
+        ]
+        for o in range(PASSES):
+            for t in range(PACK):
+                first_layer_pass(acc_last[t][:], w1q[LAST], slot_words, slot_scales, slice(SLOTS - C, SLOTS), t, o)
+        planes = keep.tile([P, PACK, C], BF16, name="planes", align_bytes=ALIGN)
+        for t in range(PACK):
+            nc.scalar.activation(out=planes[:, t, :], in_=acc_last[t][:], func=RELU)
+        hidden_last = keep.tile([P, C, PACK], BF16, name="hidden_last", align_bytes=ALIGN)
+        nc.vector.tensor_copy(
+            out=hidden_last[:].rearrange("p (c i) t -> p c t i", i=RUN), in_=planes[:].rearrange("p t (c i) -> p c t i", i=RUN)
+        )
+        hq[LAST] = quantise_hidden(hidden_last[:])
+        y_last = keep.tile([P, C], F32, name="y_last")
+        second_layer(LAST, quantise_w2(LAST, "final_words_1"), hq[LAST], y_last[:], gate_tile)
+
+        w2_words, w2_scales = quantise_w2(SHARED, w2_tag(LAST))
+        ys_head = psum_s.tile([P, 2 * OUT_PIECE], F32, name="ys_head", tag="ys_head")
+        ys_tail = psum_s.tile([P, OUT_PIECE], F32, name="ys_tail", tag="ys_tail")
+        ys = [ys_head[:, 0:OUT_PIECE], ys_head[:, OUT_PIECE : 2 * OUT_PIECE], ys_tail[:]]
         for piece in range(T // OUT_PIECE):
             cols = slice(piece * OUT_PIECE, (piece + 1) * OUT_PIECE)
             nc.tensor.matmul_mx(
-                out=accs[piece], lhsT=w2c[:].bitcast(FP8X4), lhsT_scale=w2s[:], rhs=hs_codes[:, cols].bitcast(FP8X4),
-                rhs_scale=hs_scales[:, cols], start=True, stop=True,
+                out=ys[piece],
+                lhsT=w2_words[:].bitcast(FP8X4),
+                lhsT_scale=w2_scales[:],
+                rhs=hs_words[:, cols].bitcast(FP8X4),
+                rhs_scale=hs_scales[:, cols],
+                start=True,
+                stop=True,
             )
         for piece in range(T // OUT_PIECE):
             cols = slice(piece * OUT_PIECE, (piece + 1) * OUT_PIECE)
             result = stage.tile([P, OUT_PIECE], F32, name="result")
-            nc.vector.tensor_tensor(result[:], routed[:, cols], accs[piece], ADD)
+            nc.vector.tensor_tensor(result[:], routed[:, cols], ys[piece], ADD)
             nc.sync.dma_start(out=out[:, cols], in_=result[:])

from contextlib import ExitStack

import concourse.mybir as mybir
from concourse.masks import make_identity

K, T, E, C, H, N = 1536, 768, 4, 128, 512, 128
FLOPS = 2 * (E * C + T) * (K * H + H * N)

F32 = mybir.dt.float32
BF16 = mybir.dt.bfloat16
I32 = mybir.dt.int32
U32 = mybir.dt.uint32
U16 = mybir.dt.uint16
U8 = mybir.dt.uint8
FP8X4 = mybir.dt.float8_e4m3fn_x4
COPY = mybir.ActivationFunctionType.Copy
RELU = mybir.ActivationFunctionType.Relu
MULT = mybir.AluOpType.mult
ADD = mybir.AluOpType.add

P = 128
PACK = 4
K_PASS = P * PACK
PASSES = K // K_PASS
SLOTS = E * C
SHARED = E
LAST = E - 1
PAIR = PACK // 2
QUADRANT = 32
SCALE_ROWS = 4
OFFSETS_PER_COLUMN = 16
RUN = 4
GROUPS = T // C
OUT_PIECE = 256
ALIGN = 64


def tile_moe_shr_mlp_relu_kernel(tc, x_words, x_scales, w1, w2, gate, offs, out):
    nc = tc.nc
    with ExitStack() as ctx:
        keep = ctx.enter_context(tc.tile_pool(name="keep", bufs=1))
        stage = ctx.enter_context(tc.tile_pool(name="stage", bufs=4))
        codes = ctx.enter_context(tc.tile_pool(name="codes", bufs=1))
        psum_h = ctx.enter_context(tc.psum_pool(name="psum_h", bufs=2))
        psum_y = ctx.enter_context(tc.psum_pool(name="psum_y", bufs=2))
        psum_s = ctx.enter_context(tc.psum_pool(name="psum_s", bufs=1))

        x_scale_tile = keep.tile([P, T], U8, name="x_scale_tile", align_bytes=ALIGN)
        nc.gpsimd.memset(x_scale_tile[:].bitcast(I32), 0)
        for q in range(P // QUADRANT):
            nc.scalar.dma_start(
                out=x_scale_tile[QUADRANT * q : QUADRANT * q + SCALE_ROWS * PASSES, :].bitcast(I32),
                in_=x_scales[:, SCALE_ROWS * q : SCALE_ROWS * (q + 1), :].bitcast(I32),
            )

        gate_rows = keep.tile([P, C], F32, name="gate_rows")
        nc.gpsimd.memset(gate_rows[:], 0.0)
        nc.scalar.dma_start(out=gate_rows[0:E, :], in_=gate[0, :].rearrange("(e c) -> e c", e=E))
        identity = keep.tile([P, P], F32, name="identity")
        make_identity(nc, identity[:])

        routed = keep.tile([P, T], F32, name="routed")
        nc.vector.memset(routed[:], 0.0)

        w1_raw = {}
        w2_raw = {}

        def w1_tag(e, o):
            return "w1_raw_%d_%d" % (e, o)

        def w2_tag(e):
            return "w2_raw_%d" % e

        def w1_rows(e, o):
            return w1[e, o * K_PASS : (o + 1) * K_PASS, :].rearrange("(p j) c -> p j c", j=PACK)

        def load_w1(e, o):
            w1_raw[(e, o)] = keep.tile([P, PACK, H], F32, name=w1_tag(e, o), tag=w1_tag(e, o), align_bytes=ALIGN)
            nc.sync.dma_start(out=w1_raw[(e, o)][:], in_=w1_rows(e, o))

        def load_w2(e):
            w2_raw[e] = keep.tile([P, PACK, N], F32, name=w2_tag(e), tag=w2_tag(e), align_bytes=ALIGN)
            nc.sync.dma_start(out=w2_raw[e][:], in_=w2[e].rearrange("(p j) n -> p j n", j=PACK))

        load_w1(SHARED, 0)
        offsets = keep.tile([P, SLOTS // OFFSETS_PER_COLUMN], U16, name="offsets")
        nc.sync.dma_start(offsets[:], offs)
        x_word_tile = keep.tile([P, PASSES, T], U32, name="x_word_tile", align_bytes=ALIGN)
        nc.sync.dma_start(out=x_word_tile[:].bitcast(I32), in_=x_words.rearrange("o p t r -> p o (t r)").bitcast(I32))
        token_words = [x_word_tile[:, o, :] for o in range(PASSES)]
        for o in range(1, PASSES):
            load_w1(SHARED, o)
        for e in range(LAST):
            for o in range(PASSES):
                load_w1(e, o)
            load_w2(e)
        for o in range(PASSES - 1):
            load_w1(LAST, o)
        final_raw = []
        for half in range(2):
            raw = keep.tile([P, PACK, H // 2], F32, name="final_raw_%d" % half, tag="final_raw_%d" % half, align_bytes=ALIGN)
            nc.sync.dma_start(out=raw[:], in_=w1_rows(LAST, PASSES - 1)[:, :, half * H // 2 : (half + 1) * H // 2])
            final_raw.append(raw)
        load_w2(LAST)
        load_w2(SHARED)

        def quantise(values, width, name, bufs):
            words = codes.tile([P, width], U32, name=name + "_words", align_bytes=ALIGN, bufs=bufs)
            scales = codes.tile([P, width], U8, name=name + "_scales", align_bytes=ALIGN, bufs=bufs)
            nc.vector.quantize_mx(out=words[:].bitcast(FP8X4), scales=scales[:], in_=values)
            return words, scales

        def cast_planes(raw, lower, upper, scalar_alone):
            source = raw[:].rearrange("p j (m t) -> p m j t", t=PACK)
            lower_view = lower[:].rearrange("p t m j -> p m j t")
            if scalar_alone:
                nc.scalar.activation(out=lower_view, in_=source[:, :, :, 0:PAIR], func=COPY)
            else:
                nc.vector.tensor_copy(out=lower_view, in_=source[:, :, :, 0:PAIR])
            nc.scalar.activation(out=upper[:].rearrange("p t m j -> p m j t"), in_=source[:, :, :, PAIR:PACK], func=COPY)

        def quantise_w1(e, o):
            lower = stage.tile([P, PAIR, P, PACK], BF16, name="w1_lower", align_bytes=ALIGN)
            upper = stage.tile([P, PAIR, P, PACK], BF16, name="w1_upper", align_bytes=ALIGN)
            cast_planes(w1_raw[(e, o)], lower, upper, (e, o) == (SHARED, 1))
            name, bufs = ("w1_shared", 2 * PASSES) if e == SHARED else ("w1_routed", 4 * PASSES)
            return [quantise(pair[:].rearrange("p t m j -> p (t m j)"), PAIR * P, name, bufs) for pair in (lower, upper)]

        def quantise_final_pass():
            made = []
            for pair in range(2):
                words = keep.tile([P, PAIR * P], U32, name="final_words_%d" % pair, tag="final_words_%d" % pair, align_bytes=ALIGN)
                scales = keep.tile([P, PAIR * P], U8, name="final_scales_%d" % pair, align_bytes=ALIGN)
                made.append((words, scales))
            for half in range(2):
                lower = keep.tile([P, PAIR, P // 2, PACK], BF16, name="final_lower_%d" % half, align_bytes=ALIGN)
                upper = keep.tile([P, PAIR, P // 2, PACK], BF16, name="final_upper_%d" % half, align_bytes=ALIGN)
                cast_planes(final_raw[half], lower, upper, False)
                for (words, scales), pair in zip(made, (lower, upper)):
                    for t in range(PAIR):
                        cols = slice(t * P + half * P // 2, t * P + (half + 1) * P // 2)
                        nc.vector.quantize_mx(
                            out=words[:, cols].bitcast(FP8X4), scales=scales[:, cols], in_=pair[:, t].rearrange("p m j -> p (m j)")
                        )
            return made

        def quantise_w2(e, tag):
            grouped = keep.tile([P, N, PACK], BF16, name="w2_grouped_%d" % e, tag=tag, align_bytes=ALIGN)
            nc.scalar.activation(
                out=grouped[:].rearrange("p (c i) j -> p c j i", i=RUN),
                in_=w2_raw[e][:].rearrange("p j (c i) -> p c j i", i=RUN),
                func=COPY,
            )
            return quantise(grouped[:].rearrange("p n j -> p (n j)"), N, "w2", E + 1)

        def first_layer_pass(acc, w1q, words, scales, cols, t, o):
            w_words, w_scales = w1q[o][t // PAIR]
            plane = slice((t % PAIR) * P, (t % PAIR + 1) * P)
            nc.tensor.matmul_mx(
                out=acc,
                lhsT=w_words[:, plane].bitcast(FP8X4),
                lhsT_scale=w_scales[:, plane],
                rhs=words[o][:, cols].bitcast(FP8X4),
                rhs_scale=scales[SCALE_ROWS * o : P, cols],
                start=(o == 0),
                stop=(o == PASSES - 1),
            )

        def first_layer(w1q, words, scales, cols, bank, hidden):
            acc = psum_h.tile([P, PACK, C], F32, name=bank, tag=bank)
            for t in range(PACK):
                for o in range(PASSES):
                    first_layer_pass(acc[:, t, :], w1q, words, scales, cols, t, o)
            nc.scalar.activation(out=hidden, in_=acc[:].rearrange("p t c -> p c t"), func=RELU)

        def quantise_hidden(hidden):
            return quantise(hidden.rearrange("p c t -> p (c t)"), C, "h", E)

        def second_layer(e, w2q, hq, y, gate_tile):
            acc_y = psum_y.tile([P, C], F32, name="acc_y")
            nc.tensor.matmul_mx(
                out=acc_y[:],
                lhsT=w2q[0][:].bitcast(FP8X4),
                lhsT_scale=w2q[1][:],
                rhs=hq[0][:].bitcast(FP8X4),
                rhs_scale=hq[1][:],
                start=True,
                stop=True,
            )
            nc.scalar.activation(out=y, in_=acc_y[:], func=COPY)
            entries = offsets[:, e * C // OFFSETS_PER_COLUMN : (e + 1) * C // OFFSETS_PER_COLUMN]
            nc.vector.tensor_tensor(routed[:].indirect(entries), y, gate_tile[:, e * C : (e + 1) * C], MULT)

        w1q_shared = [quantise_w1(SHARED, o) for o in range(PASSES)]
        slot_words = []
        for o in range(PASSES):
            gathered = keep.tile([P, SLOTS], U32, name="slot_words_%d" % o, align_bytes=ALIGN)
            nc.vector.tensor_copy(gathered[:], token_words[o].indirect(offsets[:]))
            slot_words.append(gathered)
        slot_scales = keep.tile([P, SLOTS], U8, name="slot_scales", tag=w1_tag(SHARED, PASSES - 1), align_bytes=ALIGN)
        nc.vector.tensor_copy(slot_scales[:], x_scale_tile[:].indirect(offsets[:]))

        gate_turned = psum_s.tile([P, P], F32, name="gate_turned", tag="ys_tail")
        nc.tensor.transpose(gate_turned[:], gate_rows[:], identity[:])
        gate_columns = keep.tile([P, E], F32, name="gate_columns", tag=w1_tag(SHARED, 1), align_bytes=ALIGN)
        nc.scalar.copy(gate_columns[:], gate_turned[:, 0:E])
        gate_spread = psum_s.tile([P, SLOTS], F32, name="gate_spread", tag="ys_head")
        for e in range(E):
            nc.tensor.transpose(gate_spread[:, e * C : (e + 1) * C], gate_columns[:, e : e + 1].to_broadcast([P, P]), identity[:])

        hs_words = keep.tile([P, T], U32, name="hs_words", align_bytes=ALIGN)
        hs_scales = keep.tile([P, T], U8, name="hs_scales", align_bytes=ALIGN)
        w1q = {}
        w2q = {}
        hq = {}
        gate_tile = None
        group = 0
        for e in range(E):
            w1q[e] = []
            for o in range(PASSES):
                w1q[e].append(quantise_final_pass() if (e, o) == (LAST, PASSES - 1) else quantise_w1(e, o))
                if o > 0 and group == GROUPS:
                    continue
                work = keep.tile([P, 2 * PACK * C], BF16, name="work_%d_%d" % (e, o), tag=w1_tag(e, o), align_bytes=ALIGN)
                hidden = work[:, 0 : PACK * C].rearrange("p (c t) -> p c t", t=PACK)
                if e > 0 and o == 0:
                    first_layer(w1q[e - 1], slot_words, slot_scales, slice((e - 1) * C, e * C), "acc_routed", hidden)
                    hq[e - 1] = quantise_hidden(hidden)
                    continue
                if e > 0 and o == 1:
                    second_layer(e - 1, w2q[e - 1], hq[e - 1], work[:, PACK * C : (PACK + 2) * C].bitcast(F32), gate_tile)
                tokens = slice(group * C, (group + 1) * C)
                first_layer(w1q_shared, token_words, x_scale_tile, tokens, "acc_shared", hidden)
                nc.vector.quantize_mx(
                    out=hs_words[:, tokens].bitcast(FP8X4), scales=hs_scales[:, tokens], in_=hidden.rearrange("p c t -> p (c t)")
                )
                group = group + 1
            if e < LAST:
                w2q[e] = quantise_w2(e, "w2_grouped_%d" % e)
            if e == 0:
                gate_tile = keep.tile([P, SLOTS], F32, name="gate_tile", tag=w2_tag(0), align_bytes=ALIGN)
                nc.scalar.copy(gate_tile[:], gate_spread[:])

        y_before = keep.tile([P, C], F32, name="y_before", tag="final_raw_1", align_bytes=ALIGN)
        second_layer(LAST - 1, w2q[LAST - 1], hq[LAST - 1], y_before[:], gate_tile)

        acc_last = [
            psum_h.tile([P, C], F32, name="acc_last_%d" % t, tag="acc_shared" if t < PAIR else "acc_routed") for t in range(PACK)
        ]
        for o in range(PASSES):
            for t in range(PACK):
                first_layer_pass(acc_last[t][:], w1q[LAST], slot_words, slot_scales, slice(SLOTS - C, SLOTS), t, o)
        planes = keep.tile([P, PACK, C], BF16, name="planes", align_bytes=ALIGN)
        for t in range(PACK):
            nc.scalar.activation(out=planes[:, t, :], in_=acc_last[t][:], func=RELU)
        hidden_last = keep.tile([P, C, PACK], BF16, name="hidden_last", align_bytes=ALIGN)
        nc.vector.tensor_copy(
            out=hidden_last[:].rearrange("p (c i) t -> p c t i", i=RUN), in_=planes[:].rearrange("p t (c i) -> p c t i", i=RUN)
        )
        hq[LAST] = quantise_hidden(hidden_last[:])
        y_last = keep.tile([P, C], F32, name="y_last")
        second_layer(LAST, quantise_w2(LAST, "final_words_1"), hq[LAST], y_last[:], gate_tile)

        w2_words, w2_scales = quantise_w2(SHARED, w2_tag(LAST))
        ys_head = psum_s.tile([P, 2 * OUT_PIECE], F32, name="ys_head", tag="ys_head")
        ys_tail = psum_s.tile([P, OUT_PIECE], F32, name="ys_tail", tag="ys_tail")
        ys = [ys_head[:, 0:OUT_PIECE], ys_head[:, OUT_PIECE : 2 * OUT_PIECE], ys_tail[:]]
        for piece in range(T // OUT_PIECE):
            cols = slice(piece * OUT_PIECE, (piece + 1) * OUT_PIECE)
            nc.tensor.matmul_mx(
                out=ys[piece],
                lhsT=w2_words[:].bitcast(FP8X4),
                lhsT_scale=w2_scales[:],
                rhs=hs_words[:, cols].bitcast(FP8X4),
                rhs_scale=hs_scales[:, cols],
                start=True,
                stop=True,
            )
        for piece in range(T // OUT_PIECE):
            cols = slice(piece * OUT_PIECE, (piece + 1) * OUT_PIECE)
            result = stage.tile([P, OUT_PIECE], F32, name="result")
            nc.vector.tensor_tensor(result[:], routed[:, cols], ys[piece], ADD)
            nc.sync.dma_start(out=out[:, cols], in_=result[:])
